import numpy as np
import ml_dtypes


def mxq(x, axis, fmt="e4m3"):
    dtype, down = {"e4m3": (ml_dtypes.float8_e4m3fn, 7), "e5m2": (ml_dtypes.float8_e5m2, 14)}[fmt]
    v = np.moveaxis(np.asarray(x, np.float32).astype(ml_dtypes.bfloat16).astype(np.float64), axis, -1)
    blocks = v.reshape(v.shape[:-1] + (-1, 32))
    amax = np.abs(blocks).max(-1, keepdims=True)
    byte = np.maximum(np.where(amax > 0, np.frexp(amax)[1] - 1 + 127, 0) - down, 1)
    scale = np.exp2(byte - 127.0)
    codes = (blocks / scale).astype(np.float32).astype(dtype).astype(np.float64)
    return np.moveaxis((codes * scale).reshape(v.shape), -1, axis)


WIDE = False


def mx_kscale(k):
    if not WIDE:
        return np.ones(k)
    levels = np.array([10, -10, 5, -5, 0])
    if k % 512:
        return np.exp2(np.random.permutation(np.resize(levels, k // 32))).repeat(32)
    a = np.empty((k // 512, 16))
    for p in range(k // 512):
        a[p, :8] = np.random.permutation(np.resize(levels, 8))
        for g in range(8):
            far = levels[np.abs(levels - a[p, g]) >= 10]
            a[p, g + 8] = far[np.random.randint(len(far))]
    return np.exp2(a.ravel()).repeat(32)


def f64(x):
    return np.asarray(x).astype(np.float64)


def striped(idx):
    return np.tile(np.asarray(idx).reshape(-1, 16).T, (8, 1)).astype(np.uint16)


def unstriped(offs):
    return offs[:16].T.reshape(-1).astype(np.int64)


E2M1 = np.array([0.0, 0.5, 1.0, 1.5, 2.0, 3.0, 4.0, 6.0, -0.0, -0.5, -1.0, -1.5, -2.0, -3.0, -4.0, -6.0])


def pack_weight(w, fmt):
    k, n = w.shape
    w = f64(np.asarray(w, np.float32).astype(ml_dtypes.bfloat16)).reshape(k // 32, 32, n)
    amax = np.abs(w).max(1)
    if fmt == "e4m3":
        byte = np.frexp(amax)[1] - 1 + 127 - 7
    else:
        mant, ex = np.frexp(amax / 6.0)
        byte = np.where(mant > 0.5, ex, ex - 1) + 127
    byte = np.clip(np.where(amax > 0, byte, 1), 1, 254)
    scaled = (w * np.exp2(127.0 - byte)[:, None, :]).reshape(k, n).astype(np.float32)
    by_word = np.ascontiguousarray(scaled.reshape(k // 512, 128, 4, n).transpose(0, 1, 3, 2))
    if fmt == "e4m3":
        words = by_word.astype(ml_dtypes.float8_e4m3fn).view(np.uint8)
    else:
        c = by_word.astype(ml_dtypes.float4_e2m1fn).view(np.uint8) & 0xF
        words = (c[..., 0::2] | (c[..., 1::2] << 4)).reshape(k // 512, 128, 2 * n)
    return np.ascontiguousarray(words), np.ascontiguousarray(byte.astype(np.uint8).reshape(k // 512, 16, n))


def unpack_weight(words, scales, fmt):
    g, _, n = scales.shape
    words = np.ascontiguousarray(words).reshape(g, 128, n, -1)
    if fmt == "e4m3":
        vals = words.view(ml_dtypes.float8_e4m3fn).astype(np.float64)
    else:
        nib = np.empty((g, 128, n, 4), np.uint8)
        nib[..., 0::2] = words & 0xF
        nib[..., 1::2] = words >> 4
        vals = E2M1[nib]
    vals = vals * np.repeat(np.exp2(scales.astype(np.float64) - 127.0), 8, axis=1)[..., None]
    return vals.transpose(0, 1, 3, 2).reshape(g * 512, n)


def bf(x):
    return np.asarray(x, np.float32).astype(ml_dtypes.bfloat16)


def planes(Y):
    r, m = Y.shape
    b = f64(bf(Y)).reshape(r // 32, 32, m)
    amax = np.abs(b).max(1)
    byte = np.clip(np.where(amax > 0, np.frexp(amax)[1] - 1 + 127 - 7, 1), 1, 254)
    codes = (b * np.exp2(127.0 - byte)[:, None, :]).reshape(r, m).astype(np.float32).astype(ml_dtypes.float8_e4m3fn).view(np.uint8)
    words = codes.reshape(r // 512, 128, 4, m).transpose(0, 1, 3, 2)
    return np.ascontiguousarray(words), np.ascontiguousarray(byte.astype(np.uint8).reshape(r // 512, 16, m))


K, D, T, I, U = 512, 512, 1024, 256, 512


def setup_inputs():
    n = np.random.standard_normal
    idx = np.random.permutation(T)[:I]
    idx2 = np.random.permutation(U)[:I]
    fk = mx_kscale(K)
    tabp = pack_weight(n((K, T)) / fk[:, None], "e4m3")
    return {
        "mat": (n((K, D)) * 1 / np.sqrt(K) * fk[:, None]).astype(np.float32),
        "tab_words": tabp[0],
        "tab_scales": tabp[1],
        "coef": (np.random.uniform(-1.0, 1.0, (1, I))).astype(np.float32),
        "anchor": (n((D, U))).astype(np.float32),
        "pull": (np.random.uniform(0.1, 0.5, (1, I))).astype(np.float32),
        "old": (n((D, T)) * 0.5).astype(np.float32),
        "offs": striped(idx),
        "offs2": striped(idx2),
    }


def reference(mat, tab_words, tab_scales, coef, anchor, pull, old, offs, offs2):
    idx = unstriped(offs)
    idx2 = unstriped(offs2)
    tabu = unpack_weight(tab_words, tab_scales, "e4m3")
    matq = mxq(f64(mat), 0, "e4m3")
    tabidxg = tabu[:, idx]
    z = matq.T @ tabidxg
    g = z * f64(coef) + f64(anchor)[:, idx2] * f64(pull)
    gf = np.zeros((D, T))
    gf[:, idx] = g
    y = f64(old) + gf
    words, scales = planes(y)
    return y, words, scales

@@ -1,0 +1,182 @@
+from contextlib import ExitStack
+
+import concourse.mybir as mybir
+from concourse.masks import make_identity
+
+K, D, T, I, U = 512, 512, 1024, 256, 512
+FLOPS = 2 * K * D * I
+
+F32 = mybir.dt.float32
+BF16 = mybir.dt.bfloat16
+I32 = mybir.dt.int32
+U32 = mybir.dt.uint32
+U16 = mybir.dt.uint16
+U8 = mybir.dt.uint8
+FP8X4 = mybir.dt.float8_e4m3fn_x4
+COPY = mybir.ActivationFunctionType.Copy
+ADD = mybir.AluOpType.add
+
+P = 128
+PACK = 4
+HALVES = I // P
+CHUNK = 256
+CHUNKS = T // CHUNK
+
+
+def tile_attend_gquadratic_pl_kernel(tc, mat, tab_words, tab_scales, coef, anchor, pull, old, offs, offs2, out_0, out_1, out_2):
+    nc = tc.nc
+    with ExitStack() as ctx:
+        sb = ctx.enter_context(tc.tile_pool(name="sb", bufs=1))
+        ps = ctx.enter_context(tc.psum_pool(name="ps", bufs=1))
+
+        offs_sb = sb.tile([P, I // 16], U16, name="offs_sb")
+        offs2_sb = sb.tile([P, I // 16], U16, name="offs2_sb")
+        nc.sync.dma_start(offs_sb[:], offs)
+        nc.sync.dma_start(offs2_sb[:], offs2)
+
+        tab_s = sb.tile([P, T], U8, name="tab_s", align_bytes=64)
+        nc.gpsimd.memset(tab_s[:].bitcast(I32), 0)
+        rows = sb.tile([P, I], F32, name="rows")
+        nc.gpsimd.memset(rows[:], 0.0)
+        for q in range(4):
+            nc.scalar.dma_start(tab_s[32 * q : 32 * q + 4, :].bitcast(I32), tab_scales[0, 4 * q : 4 * q + 4, :].bitcast(I32))
+        nc.scalar.dma_start(rows[0:1, :], coef)
+        nc.scalar.dma_start(rows[1:2, :], pull)
+
+        mat_sb = sb.tile([P, PACK, D], F32, name="mat_sb")
+        nc.sync.dma_start(mat_sb[:], mat.rearrange("(p r) d -> p r d", r=PACK))
+        tab_w = sb.tile([P, T], U32, name="tab_w", align_bytes=64)
+        nc.sync.dma_start(tab_w[:].bitcast(I32), tab_words[0].rearrange("p n t -> p (n t)").bitcast(I32))
+        anchor_rows = anchor.rearrange("(p j) u -> p j u", j=PACK)
+        anchor_sb = []
+        for h in range(2):
+            pair = sb.tile([P, 2, U], F32, name="anchor_%d" % h)
+            nc.sync.dma_start(pair[:], anchor_rows[:, 2 * h : 2 * h + 2, :])
+            anchor_sb.append(pair)
+        old_rows = old.rearrange("(p j) t -> p j t", j=PACK)
+        old_sb = []
+        for j in range(PACK):
+            plane = sb.tile([P, T], F32, name="old_%d" % j)
+            nc.sync.dma_start(plane[:], old_rows[:, j, :])
+            old_sb.append(plane)
+
+        ident = sb.tile([P, P], F32, name="ident")
+        make_identity(nc, ident[:])
+
+        windows = []
+        for j in range(PACK):
+            window = sb.tile([P, T], F32, name="window_%d" % j)
+            nc.vector.memset(window[:].bitcast(I32), 0)
+            windows.append(window)
+
+        factor_ps = ps.tile([P, HALVES, P], F32, name="factor_ps")
+        for c in range(HALVES):
+            nc.tensor.transpose(factor_ps[:, c, :], rows[:, c * P : (c + 1) * P], ident[:])
+        factors = sb.tile([P, HALVES, 2], F32, name="factors")
+        nc.scalar.activation(factors[:], factor_ps[:, :, 0:2], COPY)
+
+        got_s = sb.tile([P, I], U8, name="got_s", align_bytes=64)
+        nc.vector.tensor_copy(got_s[:], tab_s[:].indirect(offs_sb[:]))
+
+        mat_c = sb.tile([P, D], U32, name="mat_c", align_bytes=64)
+        mat_s = sb.tile([P, D], U8, name="mat_s", align_bytes=64)
+        mat_bf = []
+        for h in range(2):
+            cols = slice(h * D // 2, (h + 1) * D // 2)
+            grouped = sb.tile([P, D // 2, PACK], BF16, name="mat_bf_%d" % h, align_bytes=64)
+            dst = grouped[:].rearrange("p (c i) r -> p c r i", i=4)
+            src = mat_sb[:, :, cols].rearrange("p r (c i) -> p c r i", i=4)
+            if h == 0:
+                nc.vector.tensor_copy(dst, src)
+            else:
+                nc.scalar.copy(dst, src)
+            mat_bf.append(grouped)
+        for h in range(2):
+            cols = slice(h * D // 2, (h + 1) * D // 2)
+            nc.vector.quantize_mx(out=mat_c[:, cols].bitcast(FP8X4), scales=mat_s[:, cols], in_=mat_bf[h][:].rearrange("p c r -> p (c r)"))
+
+        got_w = sb.tile([P, I], U32, name="got_w", align_bytes=64)
+        nc.vector.tensor_copy(got_w[:], tab_w[:].indirect(offs_sb[:]))
+
+        z_ps = []
+        for c in range(HALVES):
+            slots = slice(c * P, (c + 1) * P)
+            bank = ps.tile([P, D], F32, name="z_ps_%d" % c)
+            nc.tensor.matmul_mx(out=bank[:], lhsT=got_w[:, slots].bitcast(FP8X4), lhsT_scale=got_s[:, slots],
+                                rhs=mat_c[:].bitcast(FP8X4), rhs_scale=mat_s[:], start=True, stop=True)
+            z_ps.append(bank)
+
+        picked = []
+        for j in range(PACK):
+            one = sb.tile([P, I], F32, name="picked_%d" % j)
+            nc.vector.tensor_copy(one[:], anchor_sb[j // 2][:, j % 2, :].indirect(offs2_sb[:]))
+            picked.append(one)
+
+        g_sb = []
+        zc = {}
+        for j in range(PACK):
+            h, jj = divmod(j, 2)
+            if jj == 0:
+                for c in range(HALVES):
+                    part = sb.tile([P, 2, P], F32, name="zc_%d_%d" % (c, h))
+                    src = z_ps[c][:].rearrange("i (m j) -> i j m", j=PACK)[:, 2 * h : 2 * h + 2, :]
+                    nc.scalar.activation(part[:], src, COPY, scale=factors[:, c, 0:1])
+                    zc[c, h] = part
+            bank = ps.tile([P, 2, HALVES, P], F32, name="plane_ps_%d" % j)
+            for c in range(HALVES):
+                nc.tensor.transpose(bank[:, 0, c, :], picked[j][:, c * P : (c + 1) * P], ident[:])
+            pulled = sb.tile([P, HALVES, P], F32, name="pulled_%d" % j)
+            for c in range(HALVES):
+                nc.scalar.activation(pulled[:, c, :], bank[:, 0, c, :], COPY, scale=factors[:, c, 1:2])
+            for c in range(HALVES):
+                nc.tensor.matmul(bank[:, 1, c, :], zc[c, h][:, jj, :], ident[:], start=True, stop=False, is_transpose=True)
+                nc.tensor.matmul(bank[:, 1, c, :], pulled[:, c, :], ident[:], start=False, stop=True, is_transpose=True)
+            g = sb.tile([P, I], F32, name="g_%d" % j)
+            nc.scalar.copy(g[:], bank[:, 1, :, :].rearrange("p c i -> p (c i)"))
+            g_sb.append(g)
+
+        for j in range(PACK):
+            nc.vector.tensor_copy(windows[j][:].indirect(offs_sb[:]), g_sb[j][:])
+
+        out_rows = out_0.rearrange("(p j) t -> p j t", j=PACK)
+        y = [sb.tile([P, 2, T], F32, name="y_%d" % h) for h in range(2)]
+        y_bf = [sb.tile([P, CHUNK, PACK], BF16, name="y_bf_%d" % q, align_bytes=64) for q in range(CHUNKS)]
+        y_c = sb.tile([P, T], U32, name="y_c", align_bytes=64)
+        y_s = sb.tile([P, T], U8, name="y_s", align_bytes=64)
+
+        def add(engine, j, cols):
+            engine.tensor_tensor(y[j // 2][:, j % 2, cols], old_sb[j][:, cols], windows[j][:, cols], ADD)
+
+        def store(j):
+            nc.sync.dma_start(out_rows[:, j, :], y[j // 2][:, j % 2, :])
+
+        def cast_views(h, q):
+            dst = y_bf[q][:, :, 2 * h : 2 * h + 2].rearrange("p (c i) r -> p c r i", i=4)
+            src = y[h][:, :, q * CHUNK : (q + 1) * CHUNK].rearrange("p r (c i) -> p c r i", i=4)
+            return dst, src
+
+        add(nc.gpsimd, 0, slice(0, T))
+        store(0)
+        for half in range(2):
+            add(nc.gpsimd, 1, slice(half * T // 2, (half + 1) * T // 2))
+        store(1)
+        for q in range(CHUNKS):
+            nc.scalar.copy(*cast_views(0, q))
+        add(nc.vector, 2, slice(0, T))
+        store(2)
+        for q in range(CHUNKS):
+            add(nc.vector, 3, slice(q * CHUNK, (q + 1) * CHUNK))
+        store(3)
+        for q in range(CHUNKS):
+            if q < 2:
+                nc.scalar.copy(*cast_views(1, q))
+            else:
+                nc.vector.tensor_copy(*cast_views(1, q))
+        words_out = out_1[0].rearrange("p n t -> p (n t)").bitcast(I32)
+        for q in (2, 0, 3, 1):
+            cols = slice(q * CHUNK, (q + 1) * CHUNK)
+            nc.vector.quantize_mx(out=y_c[:, cols].bitcast(FP8X4), scales=y_s[:, cols], in_=y_bf[q][:].rearrange("p c r -> p (c r)"))
+            nc.sync.dma_start(words_out[:, cols], y_c[:, cols].bitcast(I32))
+        for q in range(4):
+            queue = nc.scalar if q % 2 == 0 else nc.sync
+            queue.dma_start(out_2[0, 4 * q : 4 * q + 4, :].bitcast(I32), y_s[32 * q : 32 * q + 4, :].bitcast(I32))

@@ -21,6 +21,7 @@ PACK = 4
 HALVES = I // P
 CHUNK = 256
 CHUNKS = T // CHUNK
+SHARE = 768
 
 
 def tile_attend_gquadratic_pl_kernel(tc, mat, tab_words, tab_scales, coef, anchor, pull, old, offs, offs2, out_0, out_1, out_2):
@@ -32,27 +33,33 @@ def tile_attend_gquadratic_pl_kernel(tc, mat, tab_words, tab_scales, coef, ancho
         offs_sb = sb.tile([P, I // 16], U16, name="offs_sb")
         offs2_sb = sb.tile([P, I // 16], U16, name="offs2_sb")
         nc.sync.dma_start(offs_sb[:], offs)
-        nc.sync.dma_start(offs2_sb[:], offs2)
-
-        tab_s = sb.tile([P, T], U8, name="tab_s", align_bytes=64)
-        nc.gpsimd.memset(tab_s[:].bitcast(I32), 0)
-        rows = sb.tile([P, I], F32, name="rows")
-        nc.gpsimd.memset(rows[:], 0.0)
-        for q in range(4):
-            nc.scalar.dma_start(tab_s[32 * q : 32 * q + 4, :].bitcast(I32), tab_scales[0, 4 * q : 4 * q + 4, :].bitcast(I32))
-        nc.scalar.dma_start(rows[0:1, :], coef)
-        nc.scalar.dma_start(rows[1:2, :], pull)
 
         mat_sb = sb.tile([P, PACK, D], F32, name="mat_sb")
         nc.sync.dma_start(mat_sb[:], mat.rearrange("(p r) d -> p r d", r=PACK))
+        tab_s = sb.tile([P, T], U8, name="tab_s", align_bytes=64)
+        for q in range(4):
+            rows = tab_scales[0, 4 * q : 4 * q + 4, :].bitcast(I32)
+            nc.sync.dma_start(tab_s[32 * q : 32 * q + 32, :].bitcast(I32), rows.unsqueeze(0).to_broadcast([8, 4, T // 4]))
+        nc.sync.dma_start(offs2_sb[:], offs2)
+        anchor_rows = anchor.rearrange("(p j) u -> p j u", j=PACK)
+        anchor_sb = {}
+
+        def load_anchor(first, count):
+            part = sb.tile([P, count, U], F32, name="anchor_%d" % first)
+            nc.sync.dma_start(part[:], anchor_rows[:, first : first + count, :])
+            for j in range(count):
+                anchor_sb[first + j] = part[:, j, :]
+
         tab_w = sb.tile([P, T], U32, name="tab_w", align_bytes=64)
         nc.sync.dma_start(tab_w[:].bitcast(I32), tab_words[0].rearrange("p n t -> p (n t)").bitcast(I32))
-        anchor_rows = anchor.rearrange("(p j) u -> p j u", j=PACK)
-        anchor_sb = []
-        for h in range(2):
-            pair = sb.tile([P, 2, U], F32, name="anchor_%d" % h)
-            nc.sync.dma_start(pair[:], anchor_rows[:, 2 * h : 2 * h + 2, :])
-            anchor_sb.append(pair)
+        coef_sb = sb.tile([P, HALVES], F32, name="coef_sb")
+        pull_sb = sb.tile([P, HALVES], F32, name="pull_sb")
+        with nc.allow_non_contiguous_dma(reason="one value a partition"):
+            nc.gpsimd.dma_start(pull_sb[:], pull.rearrange("o (c p) -> p (o c)", p=P))
+            nc.gpsimd.dma_start(coef_sb[:], coef.rearrange("o (c p) -> p (o c)", p=P))
+        load_anchor(0, 1)
+        load_anchor(1, 1)
+        load_anchor(2, 2)
         old_rows = old.rearrange("(p j) t -> p j t", j=PACK)
         old_sb = []
         for j in range(PACK):
@@ -66,77 +73,67 @@ def tile_attend_gquadratic_pl_kernel(tc, mat, tab_words, tab_scales, coef, ancho
         windows = []
         for j in range(PACK):
             window = sb.tile([P, T], F32, name="window_%d" % j)
-            nc.vector.memset(window[:].bitcast(I32), 0)
+            (nc.vector if j < 3 else nc.gpsimd).memset(window[:], 0.0)
             windows.append(window)
 
-        factor_ps = ps.tile([P, HALVES, P], F32, name="factor_ps")
-        for c in range(HALVES):
-            nc.tensor.transpose(factor_ps[:, c, :], rows[:, c * P : (c + 1) * P], ident[:])
-        factors = sb.tile([P, HALVES, 2], F32, name="factors")
-        nc.scalar.activation(factors[:], factor_ps[:, :, 0:2], COPY)
+
+        mat_c = [sb.tile([P, D // 2], U32, name="mat_c_%d" % h, align_bytes=64) for h in range(2)]
+        mat_s = [sb.tile([P, D // 2], U8, name="mat_s_%d" % h, align_bytes=64) for h in range(2)]
+        mat_bf = []
+        for h in range(2):
+            grouped = sb.tile([P, 2, P, PACK], BF16, name="mat_bf_%d" % h, align_bytes=64)
+            dst = grouped[:].rearrange("p j m r -> p m j r")
+            src = mat_sb[:].rearrange("p r (m j) -> p m j r", j=PACK)[:, :, 2 * h : 2 * h + 2, :]
+            nc.scalar.copy(dst, src)
+            mat_bf.append(grouped)
+
+        def quantise_mat(h):
+            nc.vector.quantize_mx(out=mat_c[h][:].bitcast(FP8X4), scales=mat_s[h][:], in_=mat_bf[h][:].rearrange("p j m r -> p (j m r)"))
+
+        picked = []
+
+        def gather_anchor(j):
+            one = sb.tile([P, I], F32, name="picked_%d" % j)
+            nc.vector.tensor_copy(one[:], anchor_sb[j].indirect(offs2_sb[:]))
+            picked.append(one)
 
         got_s = sb.tile([P, I], U8, name="got_s", align_bytes=64)
         nc.vector.tensor_copy(got_s[:], tab_s[:].indirect(offs_sb[:]))
-
-        mat_c = sb.tile([P, D], U32, name="mat_c", align_bytes=64)
-        mat_s = sb.tile([P, D], U8, name="mat_s", align_bytes=64)
-        mat_bf = []
-        for h in range(2):
-            cols = slice(h * D // 2, (h + 1) * D // 2)
-            grouped = sb.tile([P, D // 2, PACK], BF16, name="mat_bf_%d" % h, align_bytes=64)
-            dst = grouped[:].rearrange("p (c i) r -> p c r i", i=4)
-            src = mat_sb[:, :, cols].rearrange("p r (c i) -> p c r i", i=4)
-            if h == 0:
-                nc.vector.tensor_copy(dst, src)
-            else:
-                nc.scalar.copy(dst, src)
-            mat_bf.append(grouped)
-        for h in range(2):
-            cols = slice(h * D // 2, (h + 1) * D // 2)
-            nc.vector.quantize_mx(out=mat_c[:, cols].bitcast(FP8X4), scales=mat_s[:, cols], in_=mat_bf[h][:].rearrange("p c r -> p (c r)"))
-
+        quantise_mat(0)
         got_w = sb.tile([P, I], U32, name="got_w", align_bytes=64)
         nc.vector.tensor_copy(got_w[:], tab_w[:].indirect(offs_sb[:]))
-
-        z_ps = []
-        for c in range(HALVES):
-            slots = slice(c * P, (c + 1) * P)
-            bank = ps.tile([P, D], F32, name="z_ps_%d" % c)
-            nc.tensor.matmul_mx(out=bank[:], lhsT=got_w[:, slots].bitcast(FP8X4), lhsT_scale=got_s[:, slots],
-                                rhs=mat_c[:].bitcast(FP8X4), rhs_scale=mat_s[:], start=True, stop=True)
-            z_ps.append(bank)
-
-        picked = []
-        for j in range(PACK):
-            one = sb.tile([P, I], F32, name="picked_%d" % j)
-            nc.vector.tensor_copy(one[:], anchor_sb[j // 2][:, j % 2, :].indirect(offs2_sb[:]))
-            picked.append(one)
+        gather_anchor(0)
+        quantise_mat(1)
+        for j in range(1, PACK):
+            gather_anchor(j)
 
         g_sb = []
         zc = {}
         for j in range(PACK):
             h, jj = divmod(j, 2)
-            if jj == 0:
-                for c in range(HALVES):
-                    part = sb.tile([P, 2, P], F32, name="zc_%d_%d" % (c, h))
-                    src = z_ps[c][:].rearrange("i (m j) -> i j m", j=PACK)[:, 2 * h : 2 * h + 2, :]
-                    nc.scalar.activation(part[:], src, COPY, scale=factors[:, c, 0:1])
-                    zc[c, h] = part
-            bank = ps.tile([P, 2, HALVES, P], F32, name="plane_ps_%d" % j)
+            turned = ps.tile([P, HALVES, P], F32, name="turned_ps_%d" % jj)
             for c in range(HALVES):
-                nc.tensor.transpose(bank[:, 0, c, :], picked[j][:, c * P : (c + 1) * P], ident[:])
+                nc.tensor.transpose(turned[:, c, :], picked[j][:, c * P : (c + 1) * P], ident[:])
             pulled = sb.tile([P, HALVES, P], F32, name="pulled_%d" % j)
             for c in range(HALVES):
-                nc.scalar.activation(pulled[:, c, :], bank[:, 0, c, :], COPY, scale=factors[:, c, 1:2])
+                nc.scalar.activation(pulled[:, c, :], turned[:, c, :], COPY, scale=pull_sb[:, c : c + 1])
+            if jj == 0:
+                z_ps = ps.tile([P, HALVES, 2, P], F32, name="z_ps_%d" % h, tag="z_0" if h == 0 else "g_0")
+                for c in range(HALVES):
+                    slots = slice(c * P, (c + 1) * P)
+                    nc.tensor.matmul_mx(out=z_ps[:, c, :, :].rearrange("i j m -> i (j m)"), lhsT=got_w[:, slots].bitcast(FP8X4), lhsT_scale=got_s[:, slots],
+                                        rhs=mat_c[h][:].bitcast(FP8X4), rhs_scale=mat_s[h][:], start=True, stop=True)
+                for c in range(HALVES):
+                    part = sb.tile([P, 2, P], F32, name="zc_%d_%d" % (c, h))
+                    nc.scalar.activation(part[:], z_ps[:, c, :, :], COPY, scale=coef_sb[:, c : c + 1])
+                    zc[c] = part
+            bank = ps.tile([P, HALVES, P], F32, name="g_ps_%d" % j, tag="g_%d" % j)
             for c in range(HALVES):
-                nc.tensor.matmul(bank[:, 1, c, :], zc[c, h][:, jj, :], ident[:], start=True, stop=False, is_transpose=True)
-                nc.tensor.matmul(bank[:, 1, c, :], pulled[:, c, :], ident[:], start=False, stop=True, is_transpose=True)
+                nc.tensor.matmul(bank[:, c, :], pulled[:, c, :], ident[:], start=True, stop=False, is_transpose=True)
+                nc.tensor.matmul(bank[:, c, :], zc[c][:, jj, :], ident[:], start=False, stop=True, is_transpose=True)
             g = sb.tile([P, I], F32, name="g_%d" % j)
-            nc.scalar.copy(g[:], bank[:, 1, :, :].rearrange("p c i -> p (c i)"))
+            nc.scalar.copy(g[:], bank[:].rearrange("p c i -> p (c i)"))
             g_sb.append(g)
-
-        for j in range(PACK):
-            nc.vector.tensor_copy(windows[j][:].indirect(offs_sb[:]), g_sb[j][:])
 
         out_rows = out_0.rearrange("(p j) t -> p j t", j=PACK)
         y = [sb.tile([P, 2, T], F32, name="y_%d" % h) for h in range(2)]
@@ -147,33 +144,26 @@ def tile_attend_gquadratic_pl_kernel(tc, mat, tab_words, tab_scales, coef, ancho
         def add(engine, j, cols):
             engine.tensor_tensor(y[j // 2][:, j % 2, cols], old_sb[j][:, cols], windows[j][:, cols], ADD)
 
-        def store(j):
-            nc.sync.dma_start(out_rows[:, j, :], y[j // 2][:, j % 2, :])
-
         def cast_views(h, q):
-            dst = y_bf[q][:, :, 2 * h : 2 * h + 2].rearrange("p (c i) r -> p c r i", i=4)
-            src = y[h][:, :, q * CHUNK : (q + 1) * CHUNK].rearrange("p r (c i) -> p c r i", i=4)
-            return dst, src
+            return y_bf[q][:, :, 2 * h : 2 * h + 2], y[h][:, :, q * CHUNK : (q + 1) * CHUNK].rearrange("p r c -> p c r")
 
-        add(nc.gpsimd, 0, slice(0, T))
-        store(0)
-        for half in range(2):
-            add(nc.gpsimd, 1, slice(half * T // 2, (half + 1) * T // 2))
-        store(1)
-        for q in range(CHUNKS):
-            nc.scalar.copy(*cast_views(0, q))
-        add(nc.vector, 2, slice(0, T))
-        store(2)
-        for q in range(CHUNKS):
-            add(nc.vector, 3, slice(q * CHUNK, (q + 1) * CHUNK))
-        store(3)
-        for q in range(CHUNKS):
-            if q < 2:
-                nc.scalar.copy(*cast_views(1, q))
+        for j in range(PACK):
+            nc.vector.tensor_copy(windows[j][:].indirect(offs_sb[:]), g_sb[j][:])
+            if j < PACK - 1:
+                add(nc.vector, j, slice(SHARE, T))
+                add(nc.gpsimd, j, slice(0, SHARE))
             else:
-                nc.vector.tensor_copy(*cast_views(1, q))
+                add(nc.vector, j, slice(0, T))
+            nc.sync.dma_start(out_rows[:, j, :], y[j // 2][:, j % 2, :])
+            if j == 1:
+                for q in (3, 2, 0, 1):
+                    nc.scalar.copy(*cast_views(0, q))
+        for q in (0, 1):
+            nc.scalar.copy(*cast_views(1, q))
+        for q in (3, 2):
+            nc.vector.tensor_copy(*cast_views(1, q))
         words_out = out_1[0].rearrange("p n t -> p (n t)").bitcast(I32)
-        for q in (2, 0, 3, 1):
+        for q in (3, 2, 0, 1):
             cols = slice(q * CHUNK, (q + 1) * CHUNK)
             nc.vector.quantize_mx(out=y_c[:, cols].bitcast(FP8X4), scales=y_s[:, cols], in_=y_bf[q][:].rearrange("p c r -> p (c r)"))
             nc.sync.dma_start(words_out[:, cols], y_c[:, cols].bitcast(I32))

@@ -15,13 +15,13 @@ U8 = mybir.dt.uint8
 FP8X4 = mybir.dt.float8_e4m3fn_x4
 COPY = mybir.ActivationFunctionType.Copy
 ADD = mybir.AluOpType.add
+MULT = mybir.AluOpType.mult
 
 P = 128
 PACK = 4
 HALVES = I // P
 CHUNK = 256
 CHUNKS = T // CHUNK
-SHARE = 768
 
 
 def tile_attend_gquadratic_pl_kernel(tc, mat, tab_words, tab_scales, coef, anchor, pull, old, offs, offs2, out_0, out_1, out_2):
@@ -32,34 +32,27 @@ def tile_attend_gquadratic_pl_kernel(tc, mat, tab_words, tab_scales, coef, ancho
 
         offs_sb = sb.tile([P, I // 16], U16, name="offs_sb")
         offs2_sb = sb.tile([P, I // 16], U16, name="offs2_sb")
-        nc.sync.dma_start(offs_sb[:], offs)
+        rows = sb.tile([P, P], F32, name="rows")
+        nc.gpsimd.memset(rows[:], 0.0)
 
+        nc.sync.dma_start(rows[0:HALVES, :], coef.rearrange("o (c p) -> (o c) p", p=P))
+        nc.sync.dma_start(rows[HALVES : 2 * HALVES, :], pull.rearrange("o (c p) -> (o c) p", p=P))
+        nc.sync.dma_start(offs_sb[:], offs)
         mat_sb = sb.tile([P, PACK, D], F32, name="mat_sb")
         nc.sync.dma_start(mat_sb[:], mat.rearrange("(p r) d -> p r d", r=PACK))
         tab_s = sb.tile([P, T], U8, name="tab_s", align_bytes=64)
         for q in range(4):
-            rows = tab_scales[0, 4 * q : 4 * q + 4, :].bitcast(I32)
-            nc.sync.dma_start(tab_s[32 * q : 32 * q + 32, :].bitcast(I32), rows.unsqueeze(0).to_broadcast([8, 4, T // 4]))
-        nc.sync.dma_start(offs2_sb[:], offs2)
-        anchor_rows = anchor.rearrange("(p j) u -> p j u", j=PACK)
-        anchor_sb = {}
-
-        def load_anchor(first, count):
-            part = sb.tile([P, count, U], F32, name="anchor_%d" % first)
-            nc.sync.dma_start(part[:], anchor_rows[:, first : first + count, :])
-            for j in range(count):
-                anchor_sb[first + j] = part[:, j, :]
-
+            scale_rows = tab_scales[0, 4 * q : 4 * q + 4, :].bitcast(I32)
+            nc.sync.dma_start(tab_s[32 * q : 32 * q + 32, :].bitcast(I32), scale_rows.unsqueeze(0).to_broadcast([8, 4, T // 4]))
         tab_w = sb.tile([P, T], U32, name="tab_w", align_bytes=64)
         nc.sync.dma_start(tab_w[:].bitcast(I32), tab_words[0].rearrange("p n t -> p (n t)").bitcast(I32))
-        coef_sb = sb.tile([P, HALVES], F32, name="coef_sb")
-        pull_sb = sb.tile([P, HALVES], F32, name="pull_sb")
-        with nc.allow_non_contiguous_dma(reason="one value a partition"):
-            nc.gpsimd.dma_start(pull_sb[:], pull.rearrange("o (c p) -> p (o c)", p=P))
-            nc.gpsimd.dma_start(coef_sb[:], coef.rearrange("o (c p) -> p (o c)", p=P))
-        load_anchor(0, 1)
-        load_anchor(1, 1)
-        load_anchor(2, 2)
+        nc.sync.dma_start(offs2_sb[:], offs2)
+        anchor_rows = anchor.rearrange("(p j) u -> p j u", j=PACK)
+        anchor_sb = []
+        for j in range(PACK):
+            plane = sb.tile([P, U], F32, name="anchor_%d" % j)
+            nc.sync.dma_start(plane[:], anchor_rows[:, j, :])
+            anchor_sb.append(plane)
         old_rows = old.rearrange("(p j) t -> p j t", j=PACK)
         old_sb = []
         for j in range(PACK):
@@ -71,11 +64,29 @@ def tile_attend_gquadratic_pl_kernel(tc, mat, tab_words, tab_scales, coef, ancho
         make_identity(nc, ident[:])
 
         windows = []
-        for j in range(PACK):
+        for j in range(2):
             window = sb.tile([P, T], F32, name="window_%d" % j)
-            (nc.vector if j < 3 else nc.gpsimd).memset(window[:], 0.0)
+            nc.vector.memset(window[:], 0.0)
             windows.append(window)
 
+
+        factor_ps = ps.tile([P, P], F32, name="factor_ps")
+        nc.tensor.transpose(factor_ps[:], rows[:], ident[:])
+        factors = sb.tile([P, 2 * HALVES], F32, name="factors")
+        nc.scalar.copy(factors[:], factor_ps[:, 0 : 2 * HALVES])
+        spread_ps = ps.tile([P, 2 * HALVES, P], F32, name="spread_ps")
+        for n in range(2 * HALVES):
+            nc.tensor.transpose(spread_ps[:, n, :], factors[:, n : n + 1].to_broadcast([P, P]), ident[:])
+        spread = sb.tile([P, 2 * I], F32, name="spread")
+        nc.scalar.copy(spread[:], spread_ps[:].rearrange("p n i -> p (n i)"))
+        coef_rows, pull_rows = spread[:, 0:I], spread[:, I : 2 * I]
+
+        anchor_term = []
+
+        def gather_anchor(j):
+            term = sb.tile([P, I], F32, name="anchor_term_%d" % j)
+            nc.vector.tensor_tensor(term[:], anchor_sb[j][:].indirect(offs2_sb[:]), pull_rows, MULT)
+            anchor_term.append(term)
 
         mat_c = [sb.tile([P, D // 2], U32, name="mat_c_%d" % h, align_bytes=64) for h in range(2)]
         mat_s = [sb.tile([P, D // 2], U8, name="mat_s_%d" % h, align_bytes=64) for h in range(2)]
@@ -84,18 +95,14 @@ def tile_attend_gquadratic_pl_kernel(tc, mat, tab_words, tab_scales, coef, ancho
             grouped = sb.tile([P, 2, P, PACK], BF16, name="mat_bf_%d" % h, align_bytes=64)
             dst = grouped[:].rearrange("p j m r -> p m j r")
             src = mat_sb[:].rearrange("p r (m j) -> p m j r", j=PACK)[:, :, 2 * h : 2 * h + 2, :]
-            nc.scalar.copy(dst, src)
+            if h == 0:
+                nc.vector.tensor_copy(dst, src)
+            else:
+                nc.scalar.copy(dst, src)
             mat_bf.append(grouped)
 
         def quantise_mat(h):
             nc.vector.quantize_mx(out=mat_c[h][:].bitcast(FP8X4), scales=mat_s[h][:], in_=mat_bf[h][:].rearrange("p j m r -> p (j m r)"))
-
-        picked = []
-
-        def gather_anchor(j):
-            one = sb.tile([P, I], F32, name="picked_%d" % j)
-            nc.vector.tensor_copy(one[:], anchor_sb[j].indirect(offs2_sb[:]))
-            picked.append(one)
 
         got_s = sb.tile([P, I], U8, name="got_s", align_bytes=64)
         nc.vector.tensor_copy(got_s[:], tab_s[:].indirect(offs_sb[:]))
@@ -104,36 +111,33 @@ def tile_attend_gquadratic_pl_kernel(tc, mat, tab_words, tab_scales, coef, ancho
         nc.vector.tensor_copy(got_w[:], tab_w[:].indirect(offs_sb[:]))
         gather_anchor(0)
         quantise_mat(1)
-        for j in range(1, PACK):
-            gather_anchor(j)
 
-        g_sb = []
-        zc = {}
-        for j in range(PACK):
-            h, jj = divmod(j, 2)
-            turned = ps.tile([P, HALVES, P], F32, name="turned_ps_%d" % jj)
+        z_first = ps.tile([P, I], F32, name="z_first")
+        nc.tensor.matmul_mx(out=z_first[:], lhsT=mat_c[0][:, 0:P].bitcast(FP8X4), lhsT_scale=mat_s[0][:, 0:P],
+                            rhs=got_w[:].bitcast(FP8X4), rhs_scale=got_s[:], start=True, stop=True)
+        first_term = sb.tile([P, I], F32, name="first_term")
+        nc.vector.tensor_tensor(first_term[:], z_first[:], coef_rows, MULT)
+        z_term = [first_term[:]]
+
+        def scaled_products(h, first, count):
+            cols = slice(first * P, (first + count) * P)
+            z_ps = ps.tile([P, HALVES, count * P], F32, name="z_ps_%d" % h)
             for c in range(HALVES):
-                nc.tensor.transpose(turned[:, c, :], picked[j][:, c * P : (c + 1) * P], ident[:])
-            pulled = sb.tile([P, HALVES, P], F32, name="pulled_%d" % j)
+                slots = slice(c * P, (c + 1) * P)
+                nc.tensor.matmul_mx(out=z_ps[:, c, :], lhsT=got_w[:, slots].bitcast(FP8X4), lhsT_scale=got_s[:, slots],
+                                    rhs=mat_c[h][:, cols].bitcast(FP8X4), rhs_scale=mat_s[h][:, cols], start=True, stop=True)
+            back_ps = ps.tile([P, count, HALVES, P], F32, name="back_ps_%d" % h)
             for c in range(HALVES):
-                nc.scalar.activation(pulled[:, c, :], turned[:, c, :], COPY, scale=pull_sb[:, c : c + 1])
-            if jj == 0:
-                z_ps = ps.tile([P, HALVES, 2, P], F32, name="z_ps_%d" % h, tag="z_0" if h == 0 else "g_0")
-                for c in range(HALVES):
-                    slots = slice(c * P, (c + 1) * P)
-                    nc.tensor.matmul_mx(out=z_ps[:, c, :, :].rearrange("i j m -> i (j m)"), lhsT=got_w[:, slots].bitcast(FP8X4), lhsT_scale=got_s[:, slots],
-                                        rhs=mat_c[h][:].bitcast(FP8X4), rhs_scale=mat_s[h][:], start=True, stop=True)
-                for c in range(HALVES):
-                    part = sb.tile([P, 2, P], F32, name="zc_%d_%d" % (c, h))
-                    nc.scalar.activation(part[:], z_ps[:, c, :, :], COPY, scale=coef_sb[:, c : c + 1])
-                    zc[c] = part
-            bank = ps.tile([P, HALVES, P], F32, name="g_ps_%d" % j, tag="g_%d" % j)
-            for c in range(HALVES):
-                nc.tensor.matmul(bank[:, c, :], pulled[:, c, :], ident[:], start=True, stop=False, is_transpose=True)
-                nc.tensor.matmul(bank[:, c, :], zc[c][:, jj, :], ident[:], start=False, stop=True, is_transpose=True)
-            g = sb.tile([P, I], F32, name="g_%d" % j)
-            nc.scalar.copy(g[:], bank[:].rearrange("p c i -> p (c i)"))
-            g_sb.append(g)
+                part = sb.tile([P, count, P], F32, name="zc_%d_%d" % (c, h))
+                nc.scalar.activation(part[:].rearrange("i n m -> i (n m)"), z_ps[:, c, :], COPY, scale=factors[:, c : c + 1])
+                for n in range(count):
+                    nc.tensor.transpose(back_ps[:, n, c, :], part[:, n, :], ident[:])
+            terms = sb.tile([P, count, I], F32, name="z_terms_%d" % h)
+            nc.scalar.copy(terms[:], back_ps[:].rearrange("p n c i -> p n (c i)"))
+            z_term.extend(terms[:, n, :] for n in range(count))
+
+        scaled_products(0, 1, 1)
+        scaled_products(1, 0, 2)
 
         out_rows = out_0.rearrange("(p j) t -> p j t", j=PACK)
         y = [sb.tile([P, 2, T], F32, name="y_%d" % h) for h in range(2)]
@@ -142,22 +146,31 @@ def tile_attend_gquadratic_pl_kernel(tc, mat, tab_words, tab_scales, coef, ancho
         y_s = sb.tile([P, T], U8, name="y_s", align_bytes=64)
 
         def add(engine, j, cols):
-            engine.tensor_tensor(y[j // 2][:, j % 2, cols], old_sb[j][:, cols], windows[j][:, cols], ADD)
+            engine.tensor_tensor(y[j // 2][:, j % 2, cols], old_sb[j][:, cols], windows[j % 2][:, cols], ADD)
 
         def cast_views(h, q):
             return y_bf[q][:, :, 2 * h : 2 * h + 2], y[h][:, :, q * CHUNK : (q + 1) * CHUNK].rearrange("p r c -> p c r")
 
-        for j in range(PACK):
-            nc.vector.tensor_copy(windows[j][:].indirect(offs_sb[:]), g_sb[j][:])
-            if j < PACK - 1:
-                add(nc.vector, j, slice(SHARE, T))
-                add(nc.gpsimd, j, slice(0, SHARE))
-            else:
-                add(nc.vector, j, slice(0, T))
+        def add_and_store(j):
+            add(nc.vector, j, slice(0, T))
             nc.sync.dma_start(out_rows[:, j, :], y[j // 2][:, j % 2, :])
-            if j == 1:
-                for q in (3, 2, 0, 1):
-                    nc.scalar.copy(*cast_views(0, q))
+
+        def scatter(j):
+            nc.vector.tensor_tensor(windows[j % 2][:].indirect(offs_sb[:]), z_term[j], anchor_term[j][:], ADD)
+
+        gather_anchor(1)
+        scatter(0)
+        gather_anchor(2)
+        add_and_store(0)
+        scatter(1)
+        gather_anchor(3)
+        add_and_store(1)
+        for q in (3, 2, 0, 1):
+            nc.scalar.copy(*cast_views(0, q))
+        scatter(2)
+        scatter(3)
+        add_and_store(2)
+        add_and_store(3)
         for q in (0, 1):
             nc.scalar.copy(*cast_views(1, q))
         for q in (3, 2):

from contextlib import ExitStack

import concourse.mybir as mybir
from concourse.masks import make_identity

K, D, T, I, U = 512, 512, 1024, 256, 512
FLOPS = 2 * K * D * I

F32 = mybir.dt.float32
BF16 = mybir.dt.bfloat16
I32 = mybir.dt.int32
U32 = mybir.dt.uint32
U16 = mybir.dt.uint16
U8 = mybir.dt.uint8
FP8X4 = mybir.dt.float8_e4m3fn_x4
COPY = mybir.ActivationFunctionType.Copy
ADD = mybir.AluOpType.add
MULT = mybir.AluOpType.mult

P = 128
PACK = 4
HALVES = I // P
CHUNK = 256
CHUNKS = T // CHUNK


def tile_attend_gquadratic_pl_kernel(tc, mat, tab_words, tab_scales, coef, anchor, pull, old, offs, offs2, out_0, out_1, out_2):
    nc = tc.nc
    with ExitStack() as ctx:
        sb = ctx.enter_context(tc.tile_pool(name="sb", bufs=1))
        ps = ctx.enter_context(tc.psum_pool(name="ps", bufs=1))

        offs_sb = sb.tile([P, I // 16], U16, name="offs_sb")
        offs2_sb = sb.tile([P, I // 16], U16, name="offs2_sb")
        rows = sb.tile([P, P], F32, name="rows")
        nc.gpsimd.memset(rows[:], 0.0)

        nc.sync.dma_start(rows[0:HALVES, :], coef.rearrange("o (c p) -> (o c) p", p=P))
        nc.sync.dma_start(rows[HALVES : 2 * HALVES, :], pull.rearrange("o (c p) -> (o c) p", p=P))
        nc.sync.dma_start(offs_sb[:], offs)
        mat_sb = sb.tile([P, PACK, D], F32, name="mat_sb")
        nc.sync.dma_start(mat_sb[:], mat.rearrange("(p r) d -> p r d", r=PACK))
        tab_s = sb.tile([P, T], U8, name="tab_s", align_bytes=64)
        for q in range(4):
            scale_rows = tab_scales[0, 4 * q : 4 * q + 4, :].bitcast(I32)
            nc.sync.dma_start(tab_s[32 * q : 32 * q + 32, :].bitcast(I32), scale_rows.unsqueeze(0).to_broadcast([8, 4, T // 4]))
        tab_w = sb.tile([P, T], U32, name="tab_w", align_bytes=64)
        nc.sync.dma_start(tab_w[:].bitcast(I32), tab_words[0].rearrange("p n t -> p (n t)").bitcast(I32))
        nc.sync.dma_start(offs2_sb[:], offs2)
        anchor_rows = anchor.rearrange("(p j) u -> p j u", j=PACK)
        anchor_sb = []
        for j in range(PACK):
            plane = sb.tile([P, U], F32, name="anchor_%d" % j)
            nc.sync.dma_start(plane[:], anchor_rows[:, j, :])
            anchor_sb.append(plane)
        old_rows = old.rearrange("(p j) t -> p j t", j=PACK)
        old_sb = []
        for j in range(PACK):
            plane = sb.tile([P, T], F32, name="old_%d" % j)
            nc.sync.dma_start(plane[:], old_rows[:, j, :])
            old_sb.append(plane)

        ident = sb.tile([P, P], F32, name="ident")
        make_identity(nc, ident[:])

        windows = []
        for j in range(2):
            window = sb.tile([P, T], F32, name="window_%d" % j)
            nc.vector.memset(window[:], 0.0)
            windows.append(window)


        factor_ps = ps.tile([P, P], F32, name="factor_ps")
        nc.tensor.transpose(factor_ps[:], rows[:], ident[:])
        factors = sb.tile([P, 2 * HALVES], F32, name="factors")
        nc.scalar.copy(factors[:], factor_ps[:, 0 : 2 * HALVES])
        spread_ps = ps.tile([P, 2 * HALVES, P], F32, name="spread_ps")
        for n in range(2 * HALVES):
            nc.tensor.transpose(spread_ps[:, n, :], factors[:, n : n + 1].to_broadcast([P, P]), ident[:])
        spread = sb.tile([P, 2 * I], F32, name="spread")
        nc.scalar.copy(spread[:], spread_ps[:].rearrange("p n i -> p (n i)"))
        coef_rows, pull_rows = spread[:, 0:I], spread[:, I : 2 * I]

        anchor_term = []

        def gather_anchor(j):
            term = sb.tile([P, I], F32, name="anchor_term_%d" % j)
            nc.vector.tensor_tensor(term[:], anchor_sb[j][:].indirect(offs2_sb[:]), pull_rows, MULT)
            anchor_term.append(term)

        mat_c = [sb.tile([P, D // 2], U32, name="mat_c_%d" % h, align_bytes=64) for h in range(2)]
        mat_s = [sb.tile([P, D // 2], U8, name="mat_s_%d" % h, align_bytes=64) for h in range(2)]
        mat_bf = []
        for h in range(2):
            grouped = sb.tile([P, 2, P, PACK], BF16, name="mat_bf_%d" % h, align_bytes=64)
            dst = grouped[:].rearrange("p j m r -> p m j r")
            src = mat_sb[:].rearrange("p r (m j) -> p m j r", j=PACK)[:, :, 2 * h : 2 * h + 2, :]
            if h == 0:
                nc.vector.tensor_copy(dst, src)
            else:
                nc.scalar.copy(dst, src)
            mat_bf.append(grouped)

        def quantise_mat(h):
            nc.vector.quantize_mx(out=mat_c[h][:].bitcast(FP8X4), scales=mat_s[h][:], in_=mat_bf[h][:].rearrange("p j m r -> p (j m r)"))

        got_s = sb.tile([P, I], U8, name="got_s", align_bytes=64)
        nc.vector.tensor_copy(got_s[:], tab_s[:].indirect(offs_sb[:]))
        quantise_mat(0)
        got_w = sb.tile([P, I], U32, name="got_w", align_bytes=64)
        nc.vector.tensor_copy(got_w[:], tab_w[:].indirect(offs_sb[:]))
        gather_anchor(0)
        quantise_mat(1)

        z_first = ps.tile([P, I], F32, name="z_first")
        nc.tensor.matmul_mx(out=z_first[:], lhsT=mat_c[0][:, 0:P].bitcast(FP8X4), lhsT_scale=mat_s[0][:, 0:P],
                            rhs=got_w[:].bitcast(FP8X4), rhs_scale=got_s[:], start=True, stop=True)
        first_term = sb.tile([P, I], F32, name="first_term")
        nc.vector.tensor_tensor(first_term[:], z_first[:], coef_rows, MULT)
        z_term = [first_term[:]]

        def scaled_products(h, first, count):
            cols = slice(first * P, (first + count) * P)
            z_ps = ps.tile([P, HALVES, count * P], F32, name="z_ps_%d" % h)
            for c in range(HALVES):
                slots = slice(c * P, (c + 1) * P)
                nc.tensor.matmul_mx(out=z_ps[:, c, :], lhsT=got_w[:, slots].bitcast(FP8X4), lhsT_scale=got_s[:, slots],
                                    rhs=mat_c[h][:, cols].bitcast(FP8X4), rhs_scale=mat_s[h][:, cols], start=True, stop=True)
            back_ps = ps.tile([P, count, HALVES, P], F32, name="back_ps_%d" % h)
            for c in range(HALVES):
                part = sb.tile([P, count, P], F32, name="zc_%d_%d" % (c, h))
                nc.scalar.activation(part[:].rearrange("i n m -> i (n m)"), z_ps[:, c, :], COPY, scale=factors[:, c : c + 1])
                for n in range(count):
                    nc.tensor.transpose(back_ps[:, n, c, :], part[:, n, :], ident[:])
            terms = sb.tile([P, count, I], F32, name="z_terms_%d" % h)
            nc.scalar.copy(terms[:], back_ps[:].rearrange("p n c i -> p n (c i)"))
            z_term.extend(terms[:, n, :] for n in range(count))

        scaled_products(0, 1, 1)
        scaled_products(1, 0, 2)

        out_rows = out_0.rearrange("(p j) t -> p j t", j=PACK)
        y = [sb.tile([P, 2, T], F32, name="y_%d" % h) for h in range(2)]
        y_bf = [sb.tile([P, CHUNK, PACK], BF16, name="y_bf_%d" % q, align_bytes=64) for q in range(CHUNKS)]
        y_c = sb.tile([P, T], U32, name="y_c", align_bytes=64)
        y_s = sb.tile([P, T], U8, name="y_s", align_bytes=64)

        def add(engine, j, cols):
            engine.tensor_tensor(y[j // 2][:, j % 2, cols], old_sb[j][:, cols], windows[j % 2][:, cols], ADD)

        def cast_views(h, q):
            return y_bf[q][:, :, 2 * h : 2 * h + 2], y[h][:, :, q * CHUNK : (q + 1) * CHUNK].rearrange("p r c -> p c r")

        def add_and_store(j):
            add(nc.vector, j, slice(0, T))
            nc.sync.dma_start(out_rows[:, j, :], y[j // 2][:, j % 2, :])

        def scatter(j):
            nc.vector.tensor_tensor(windows[j % 2][:].indirect(offs_sb[:]), z_term[j], anchor_term[j][:], ADD)

        gather_anchor(1)
        scatter(0)
        gather_anchor(2)
        add_and_store(0)
        scatter(1)
        gather_anchor(3)
        add_and_store(1)
        for q in (3, 2, 0, 1):
            nc.scalar.copy(*cast_views(0, q))
        scatter(2)
        scatter(3)
        add_and_store(2)
        add_and_store(3)
        for q in (0, 1):
            nc.scalar.copy(*cast_views(1, q))
        for q in (3, 2):
            nc.vector.tensor_copy(*cast_views(1, q))
        words_out = out_1[0].rearrange("p n t -> p (n t)").bitcast(I32)
        for q in (3, 2, 0, 1):
            cols = slice(q * CHUNK, (q + 1) * CHUNK)
            nc.vector.quantize_mx(out=y_c[:, cols].bitcast(FP8X4), scales=y_s[:, cols], in_=y_bf[q][:].rearrange("p c r -> p (c r)"))
            nc.sync.dma_start(words_out[:, cols], y_c[:, cols].bitcast(I32))
        for q in range(4):
            queue = nc.scalar if q % 2 == 0 else nc.sync
            queue.dma_start(out_2[0, 4 * q : 4 * q + 4, :].bitcast(I32), y_s[32 * q : 32 * q + 4, :].bitcast(I32))
